import numpy as np
import ml_dtypes

BF16 = ml_dtypes.bfloat16


def bf(x):
    return np.asarray(x, np.float32).astype(BF16)


def f32(x):
    return np.asarray(x, np.float32)


def f64(x):
    return np.asarray(x).astype(np.float64)


def striped(idx):
    return np.concatenate([l.reshape(-1, 16).T for l in idx])


def rows(idx, k):
    return np.tile(np.repeat(idx, 16, axis=0), (k // (16 * 8), 1))


def look(tab, idx):
    return np.take_along_axis(f64(tab), rows(idx, len(tab)), axis=1)


K, S, V, N = 256, 2048, 2048, 2048


def setup_inputs():
    return {"tab": f32(np.random.standard_normal((2, K, S))), "y": f32(np.random.standard_normal((K, V))), "offs": striped(np.stack([np.random.permutation(S)[:N] for _ in range(8)]))}


def reference(tab, y, offs):
    idx = np.stack([g.T.reshape(-1) for g in np.split(offs, 8)])
    x = (look(tab[0], idx) * f64(y)) * (np.tanh(look(tab[1], idx)))
    return x

@@ -1,0 +1,42 @@
+import concourse.mybir as mybir
+
+F32 = mybir.dt.float32
+U16 = mybir.dt.uint16
+mult = mybir.AluOpType.mult
+tanh = mybir.ActivationFunctionType.Tanh
+
+P = 128
+PIECE = 512
+
+
+def tile_lookup_vg_multanh_out_kernel(tc, tab, y, offs, out):
+    nc = tc.nc
+    rows, n = y.shape
+    places = tab.shape[2]
+    pieces = n // PIECE
+    cols = PIECE // 16
+    with (
+        tc.tile_pool(name="held", bufs=1) as held,
+        tc.tile_pool(name="blocks", bufs=2) as blocks,
+        tc.tile_pool(name="work", bufs=2 * pieces) as work,
+    ):
+        lists = held.tile([P, n // 16], U16)
+        nc.sync.dma_start(lists[:], offs)
+        for b in range(rows // P):
+            block = slice(b * P, (b + 1) * P)
+            values = blocks.tile([P, places], F32)
+            stream = blocks.tile([P, n], F32)
+            gates = blocks.tile([P, places], F32)
+            nc.sync.dma_start(values[:], tab[0, block, :])
+            nc.sync.dma_start(stream[:], y[block, :])
+            nc.sync.dma_start(gates[:], tab[1, block, :])
+            for k in range(pieces):
+                piece = slice(k * PIECE, (k + 1) * PIECE)
+                entries = lists[:, k * cols : (k + 1) * cols]
+                scaled = work.tile([P, PIECE], F32)
+                gate = work.tile([P, PIECE], F32)
+                gated = work.tile([P, PIECE], F32)
+                nc.vector.tensor_tensor(scaled[:], values[:].indirect(entries), stream[:, piece], mult)
+                nc.scalar.activation(gate[:], gates[:].indirect(entries), tanh)
+                nc.vector.tensor_tensor(gated[:], scaled[:], gate[:], mult)
+                nc.sync.dma_start(out[block, piece], gated[:])

@@ -27,9 +27,11 @@ def tile_lookup_vg_multanh_out_kernel(tc, tab, y, offs, out):
             values = blocks.tile([P, places], F32)
             stream = blocks.tile([P, n], F32)
             gates = blocks.tile([P, places], F32)
+            half = n // 2
             nc.sync.dma_start(values[:], tab[0, block, :])
-            nc.sync.dma_start(stream[:], y[block, :])
+            nc.sync.dma_start(stream[:, :half], y[block, :half])
             nc.sync.dma_start(gates[:], tab[1, block, :])
+            nc.sync.dma_start(stream[:, half:], y[block, half:])
             for k in range(pieces):
                 piece = slice(k * PIECE, (k + 1) * PIECE)
                 entries = lists[:, k * cols : (k + 1) * cols]

@@ -7,6 +7,7 @@ tanh = mybir.ActivationFunctionType.Tanh
 
 P = 128
 PIECE = 512
+LAG = 1
 
 
 def tile_lookup_vg_multanh_out_kernel(tc, tab, y, offs, out):
@@ -15,6 +16,7 @@ def tile_lookup_vg_multanh_out_kernel(tc, tab, y, offs, out):
     places = tab.shape[2]
     pieces = n // PIECE
     cols = PIECE // 16
+    half = n // 2
     with (
         tc.tile_pool(name="held", bufs=1) as held,
         tc.tile_pool(name="blocks", bufs=2) as blocks,
@@ -22,23 +24,46 @@ def tile_lookup_vg_multanh_out_kernel(tc, tab, y, offs, out):
     ):
         lists = held.tile([P, n // 16], U16)
         nc.sync.dma_start(lists[:], offs)
-        for b in range(rows // P):
+
+        warm = held.tile([P, 1], F32)
+        nc.gpsimd.memset(warm[:], 0.0)
+        nc.scalar.activation(warm[:], warm[:], tanh)
+
+        def load(b):
             block = slice(b * P, (b + 1) * P)
             values = blocks.tile([P, places], F32)
             stream = blocks.tile([P, n], F32)
             gates = blocks.tile([P, places], F32)
-            half = n // 2
             nc.sync.dma_start(values[:], tab[0, block, :])
             nc.sync.dma_start(stream[:, :half], y[block, :half])
             nc.sync.dma_start(gates[:], tab[1, block, :])
             nc.sync.dma_start(stream[:, half:], y[block, half:])
-            for k in range(pieces):
-                piece = slice(k * PIECE, (k + 1) * PIECE)
-                entries = lists[:, k * cols : (k + 1) * cols]
-                scaled = work.tile([P, PIECE], F32)
-                gate = work.tile([P, PIECE], F32)
-                gated = work.tile([P, PIECE], F32)
-                nc.vector.tensor_tensor(scaled[:], values[:].indirect(entries), stream[:, piece], mult)
-                nc.scalar.activation(gate[:], gates[:].indirect(entries), tanh)
-                nc.vector.tensor_tensor(gated[:], scaled[:], gate[:], mult)
-                nc.sync.dma_start(out[block, piece], gated[:])
+            return values, stream, gates
+
+        def look_up(tables, k):
+            values, stream, gates = tables
+            entries = lists[:, k * cols : (k + 1) * cols]
+            scaled = work.tile([P, PIECE], F32)
+            gate = work.tile([P, PIECE], F32)
+            nc.vector.tensor_tensor(
+                scaled[:], values[:].indirect(entries), stream[:, k * PIECE : (k + 1) * PIECE], mult
+            )
+            nc.scalar.activation(gate[:], gates[:].indirect(entries), tanh)
+            return scaled, gate
+
+        def join(picked, b, k):
+            scaled, gate = picked
+            gated = work.tile([P, PIECE], F32)
+            nc.vector.tensor_tensor(gated[:], scaled[:], gate[:], mult)
+            nc.sync.dma_start(out[b * P : (b + 1) * P, k * PIECE : (k + 1) * PIECE], gated[:])
+
+        tables = [load(b) for b in range(rows // P)]
+        work_list = [(b, k) for b in range(rows // P) for k in range(pieces)]
+        picked = {}
+        for u, (b, k) in enumerate(work_list):
+            picked[b, k] = look_up(tables[b], k)
+            if u >= LAG:
+                earlier = work_list[u - LAG]
+                join(picked[earlier], *earlier)
+        for last in work_list[len(work_list) - LAG :]:
+            join(picked[last], *last)

@@ -8,6 +8,7 @@ tanh = mybir.ActivationFunctionType.Tanh
 P = 128
 PIECE = 512
 LAG = 1
+EARLY = 2
 
 
 def tile_lookup_vg_multanh_out_kernel(tc, tab, y, offs, out):
@@ -16,7 +17,6 @@ def tile_lookup_vg_multanh_out_kernel(tc, tab, y, offs, out):
     places = tab.shape[2]
     pieces = n // PIECE
     cols = PIECE // 16
-    half = n // 2
     with (
         tc.tile_pool(name="held", bufs=1) as held,
         tc.tile_pool(name="blocks", bufs=2) as blocks,
@@ -35,9 +35,11 @@ def tile_lookup_vg_multanh_out_kernel(tc, tab, y, offs, out):
             stream = blocks.tile([P, n], F32)
             gates = blocks.tile([P, places], F32)
             nc.sync.dma_start(values[:], tab[0, block, :])
-            nc.sync.dma_start(stream[:, :half], y[block, :half])
-            nc.sync.dma_start(gates[:], tab[1, block, :])
-            nc.sync.dma_start(stream[:, half:], y[block, half:])
+            for k in range(pieces):
+                if k == EARLY:
+                    nc.sync.dma_start(gates[:], tab[1, block, :])
+                piece = slice(k * PIECE, (k + 1) * PIECE)
+                nc.sync.dma_start(stream[:, piece], y[block, piece])
             return values, stream, gates
 
         def look_up(tables, k):

@@ -7,33 +7,33 @@ tanh = mybir.ActivationFunctionType.Tanh
 
 P = 128
 PIECE = 512
-LAG = 1
-EARLY = 2
+COLS = PIECE // 16
+EARLY = 1
 
 
 def tile_lookup_vg_multanh_out_kernel(tc, tab, y, offs, out):
     nc = tc.nc
     rows, n = y.shape
     places = tab.shape[2]
+    blocks = rows // P
     pieces = n // PIECE
-    cols = PIECE // 16
     with (
         tc.tile_pool(name="held", bufs=1) as held,
-        tc.tile_pool(name="blocks", bufs=2) as blocks,
-        tc.tile_pool(name="work", bufs=2 * pieces) as work,
+        tc.tile_pool(name="inputs", bufs=blocks) as inputs,
+        tc.tile_pool(name="results", bufs=blocks * pieces) as results,
     ):
         lists = held.tile([P, n // 16], U16)
         nc.sync.dma_start(lists[:], offs)
 
-        warm = held.tile([P, 1], F32)
-        nc.gpsimd.memset(warm[:], 0.0)
-        nc.scalar.activation(warm[:], warm[:], tanh)
+        zeros = held.tile([P, 1], F32)
+        nc.gpsimd.memset(zeros[:], 0.0)
+        nc.scalar.activation(zeros[:], zeros[:], tanh)
 
         def load(b):
             block = slice(b * P, (b + 1) * P)
-            values = blocks.tile([P, places], F32)
-            stream = blocks.tile([P, n], F32)
-            gates = blocks.tile([P, places], F32)
+            values = inputs.tile([P, places], F32)
+            stream = inputs.tile([P, n], F32)
+            gates = inputs.tile([P, places], F32)
             nc.sync.dma_start(values[:], tab[0, block, :])
             for k in range(pieces):
                 if k == EARLY:
@@ -42,30 +42,27 @@ def tile_lookup_vg_multanh_out_kernel(tc, tab, y, offs, out):
                 nc.sync.dma_start(stream[:, piece], y[block, piece])
             return values, stream, gates
 
-        def look_up(tables, k):
-            values, stream, gates = tables
-            entries = lists[:, k * cols : (k + 1) * cols]
-            scaled = work.tile([P, PIECE], F32)
-            gate = work.tile([P, PIECE], F32)
-            nc.vector.tensor_tensor(
-                scaled[:], values[:].indirect(entries), stream[:, k * PIECE : (k + 1) * PIECE], mult
-            )
+        def look_up(values, stream, gates, k):
+            piece = slice(k * PIECE, (k + 1) * PIECE)
+            entries = lists[:, k * COLS : (k + 1) * COLS]
+            scaled = results.tile([P, PIECE], F32)
+            gate = results.tile([P, PIECE], F32)
+            nc.vector.tensor_tensor(scaled[:], values[:].indirect(entries), stream[:, piece], mult)
             nc.scalar.activation(gate[:], gates[:].indirect(entries), tanh)
             return scaled, gate
 
-        def join(picked, b, k):
-            scaled, gate = picked
-            gated = work.tile([P, PIECE], F32)
+        def join(scaled, gate, b, k):
+            gated = results.tile([P, PIECE], F32)
             nc.vector.tensor_tensor(gated[:], scaled[:], gate[:], mult)
             nc.sync.dma_start(out[b * P : (b + 1) * P, k * PIECE : (k + 1) * PIECE], gated[:])
 
-        tables = [load(b) for b in range(rows // P)]
-        work_list = [(b, k) for b in range(rows // P) for k in range(pieces)]
-        picked = {}
-        for u, (b, k) in enumerate(work_list):
-            picked[b, k] = look_up(tables[b], k)
-            if u >= LAG:
-                earlier = work_list[u - LAG]
-                join(picked[earlier], *earlier)
-        for last in work_list[len(work_list) - LAG :]:
-            join(picked[last], *last)
+        loaded = [load(b) for b in range(blocks)]
+
+        waiting = None
+        for b in range(blocks):
+            for k in range(pieces):
+                scaled, gate = look_up(*loaded[b], k)
+                if waiting:
+                    join(*waiting)
+                waiting = (scaled, gate, b, k)
+        join(*waiting)

import concourse.mybir as mybir

F32 = mybir.dt.float32
U16 = mybir.dt.uint16
mult = mybir.AluOpType.mult
tanh = mybir.ActivationFunctionType.Tanh

P = 128
PIECE = 512
COLS = PIECE // 16
EARLY = 1


def tile_lookup_vg_multanh_out_kernel(tc, tab, y, offs, out):
    nc = tc.nc
    rows, n = y.shape
    places = tab.shape[2]
    blocks = rows // P
    pieces = n // PIECE
    with (
        tc.tile_pool(name="held", bufs=1) as held,
        tc.tile_pool(name="inputs", bufs=blocks) as inputs,
        tc.tile_pool(name="results", bufs=blocks * pieces) as results,
    ):
        lists = held.tile([P, n // 16], U16)
        nc.sync.dma_start(lists[:], offs)

        zeros = held.tile([P, 1], F32)
        nc.gpsimd.memset(zeros[:], 0.0)
        nc.scalar.activation(zeros[:], zeros[:], tanh)

        def load(b):
            block = slice(b * P, (b + 1) * P)
            values = inputs.tile([P, places], F32)
            stream = inputs.tile([P, n], F32)
            gates = inputs.tile([P, places], F32)
            nc.sync.dma_start(values[:], tab[0, block, :])
            for k in range(pieces):
                if k == EARLY:
                    nc.sync.dma_start(gates[:], tab[1, block, :])
                piece = slice(k * PIECE, (k + 1) * PIECE)
                nc.sync.dma_start(stream[:, piece], y[block, piece])
            return values, stream, gates

        def look_up(values, stream, gates, k):
            piece = slice(k * PIECE, (k + 1) * PIECE)
            entries = lists[:, k * COLS : (k + 1) * COLS]
            scaled = results.tile([P, PIECE], F32)
            gate = results.tile([P, PIECE], F32)
            nc.vector.tensor_tensor(scaled[:], values[:].indirect(entries), stream[:, piece], mult)
            nc.scalar.activation(gate[:], gates[:].indirect(entries), tanh)
            return scaled, gate

        def join(scaled, gate, b, k):
            gated = results.tile([P, PIECE], F32)
            nc.vector.tensor_tensor(gated[:], scaled[:], gate[:], mult)
            nc.sync.dma_start(out[b * P : (b + 1) * P, k * PIECE : (k + 1) * PIECE], gated[:])

        loaded = [load(b) for b in range(blocks)]

        waiting = None
        for b in range(blocks):
            for k in range(pieces):
                scaled, gate = look_up(*loaded[b], k)
                if waiting:
                    join(*waiting)
                waiting = (scaled, gate, b, k)
        join(*waiting)
